import numpy as np
import ml_dtypes


def mxq(x, axis, fmt="e4m3"):
    dtype, down = {"e4m3": (ml_dtypes.float8_e4m3fn, 7), "e5m2": (ml_dtypes.float8_e5m2, 14)}[fmt]
    v = np.moveaxis(np.asarray(x, np.float32).astype(ml_dtypes.bfloat16).astype(np.float64), axis, -1)
    blocks = v.reshape(v.shape[:-1] + (-1, 32))
    amax = np.abs(blocks).max(-1, keepdims=True)
    byte = np.maximum(np.where(amax > 0, np.frexp(amax)[1] - 1 + 127, 0) - down, 1)
    scale = np.exp2(byte - 127.0)
    codes = (blocks / scale).astype(np.float32).astype(dtype).astype(np.float64)
    return np.moveaxis((codes * scale).reshape(v.shape), -1, axis)


WIDE = False


def mx_kscale(k):
    if not WIDE:
        return np.ones(k)
    levels = np.array([10, -10, 5, -5, 0])
    if k % 512:
        return np.exp2(np.random.permutation(np.resize(levels, k // 32))).repeat(32)
    a = np.empty((k // 512, 16))
    for p in range(k // 512):
        a[p, :8] = np.random.permutation(np.resize(levels, 8))
        for g in range(8):
            far = levels[np.abs(levels - a[p, g]) >= 10]
            a[p, g + 8] = far[np.random.randint(len(far))]
    return np.exp2(a.ravel()).repeat(32)


def f64(x):
    return np.asarray(x).astype(np.float64)


def striped8(idx):
    return np.asarray(idx).reshape(8, -1, 16).transpose(0, 2, 1).reshape(128, -1).astype(np.uint16)


def unstriped8(offs):
    return offs.reshape(8, 16, -1).transpose(0, 2, 1).reshape(8, -1).astype(np.int64)


def pick8(x, idx, run):
    r = np.arange(len(x))
    return x[r[:, None], idx[r % (8 * run) // run]]


E2M1 = np.array([0.0, 0.5, 1.0, 1.5, 2.0, 3.0, 4.0, 6.0, -0.0, -0.5, -1.0, -1.5, -2.0, -3.0, -4.0, -6.0])


def pack_weight(w, fmt):
    k, n = w.shape
    w = f64(np.asarray(w, np.float32).astype(ml_dtypes.bfloat16)).reshape(k // 32, 32, n)
    amax = np.abs(w).max(1)
    if fmt == "e4m3":
        byte = np.frexp(amax)[1] - 1 + 127 - 7
    else:
        mant, ex = np.frexp(amax / 6.0)
        byte = np.where(mant > 0.5, ex, ex - 1) + 127
    byte = np.clip(np.where(amax > 0, byte, 1), 1, 254)
    scaled = (w * np.exp2(127.0 - byte)[:, None, :]).reshape(k, n).astype(np.float32)
    by_word = np.ascontiguousarray(scaled.reshape(k // 512, 128, 4, n).transpose(0, 1, 3, 2))
    if fmt == "e4m3":
        words = by_word.astype(ml_dtypes.float8_e4m3fn).view(np.uint8)
    else:
        c = by_word.astype(ml_dtypes.float4_e2m1fn).view(np.uint8) & 0xF
        words = (c[..., 0::2] | (c[..., 1::2] << 4)).reshape(k // 512, 128, 2 * n)
    return np.ascontiguousarray(words), np.ascontiguousarray(byte.astype(np.uint8).reshape(k // 512, 16, n))


def unpack_weight(words, scales, fmt):
    g, _, n = scales.shape
    words = np.ascontiguousarray(words).reshape(g, 128, n, -1)
    if fmt == "e4m3":
        vals = words.view(ml_dtypes.float8_e4m3fn).astype(np.float64)
    else:
        nib = np.empty((g, 128, n, 4), np.uint8)
        nib[..., 0::2] = words & 0xF
        nib[..., 1::2] = words >> 4
        vals = E2M1[nib]
    vals = vals * np.repeat(np.exp2(scales.astype(np.float64) - 127.0), 8, axis=1)[..., None]
    return vals.transpose(0, 1, 3, 2).reshape(g * 512, n)


D, E, T, Q, I = 512, 512, 1024, 128, 512


def setup_inputs():
    n = np.random.standard_normal
    idx = np.stack([np.random.permutation(T)[:I] for _ in range(8)])
    fd = mx_kscale(D)
    ft = mx_kscale(T)
    keysp = pack_weight(n((D, T)) / fd[:, None], "e4m3")
    return {
        "query": (n((D, Q)) * 1.0 / np.sqrt(D) * fd[:, None]).astype(np.float32),
        "keys_words": keysp[0],
        "keys_scales": keysp[1],
        "th": (np.random.uniform(-0.5, 0.5, (Q, 1))).astype(np.float32),
        "reserve": (np.random.uniform(20.0, 60.0, (Q, 1))).astype(np.float32),
        "ground": (np.random.uniform(0.0, 0.004, (Q, T))).astype(np.float32),
        "fac": (np.random.uniform(8.0, 32.0, (1, T)) * ft).astype(np.float32),
        "vals": (n((T, E)) / ft[:, None]).astype(np.float32),
        "offs": striped8(idx),
    }


def reference(query, keys_words, keys_scales, th, reserve, ground, fac, vals, offs):
    idx = unstriped8(offs)
    keysu = unpack_weight(keys_words, keys_scales, "e4m3")
    queryq = mxq(f64(query), 0, "e4m3")
    a = queryq.T @ keysu
    b = np.maximum(pick8(a, idx, 16) - f64(th), 0.0)
    u = b / (np.sum(b, axis=1, keepdims=True) + f64(reserve))
    uf = np.zeros((Q, T))
    uf[np.arange(Q)[:, None], idx[np.arange(Q) % 128 // 16]] = u
    wg = (uf + f64(ground)) * f64(fac)
    wt = wg.T
    wtq = mxq(wt, 0, "e4m3")
    valsq = mxq(f64(vals), 0, "e4m3")
    o = wtq.T @ valsq
    return o

@@ -1,0 +1,213 @@
+from contextlib import ExitStack
+
+import concourse.mybir as mybir
+from concourse.masks import make_identity
+
+D, E, T, Q, SLOTS = 512, 512, 1024, 128, 512
+FLOPS = 2 * Q * D * T + 2 * Q * T * E
+
+F32 = mybir.dt.float32
+BF16 = mybir.dt.bfloat16
+I32 = mybir.dt.int32
+U32 = mybir.dt.uint32
+U16 = mybir.dt.uint16
+U8 = mybir.dt.uint8
+FP8X4 = mybir.dt.float8_e4m3fn_x4
+ALU = mybir.AluOpType
+ACT = mybir.ActivationFunctionType
+
+P = 128
+PACK = 4
+K_PASS = P * PACK
+PASSES = T // K_PASS
+SCORE_N = 256
+SCORE_TILES = T // SCORE_N
+OUT_N = 256
+OUT_TILES = E // OUT_N
+
+
+def tile_attend_spotlight_heads_kernel(tc, query, keys_words, keys_scales, th, reserve, ground, fac, vals, offs, out):
+    nc = tc.nc
+    with ExitStack() as ctx:
+        sb = ctx.enter_context(tc.tile_pool(name="sb", bufs=1))
+        psum = ctx.enter_context(tc.psum_pool(name="psum", bufs=1))
+
+        offsets = sb.tile([P, SLOTS // 16], U16, name="offsets")
+        q_raw = sb.tile([P, PACK, Q], F32, name="q_raw")
+        key_codes = [sb.tile([P, K_PASS], U32, name=f"key_codes{h}", align_bytes=64) for h in range(2)]
+        key_scales = sb.tile([P, SCORE_N], U8, name="key_scales", align_bytes=64)
+        th_col = sb.tile([P, 1], F32, name="th_col")
+        reserve_col = sb.tile([P, 1], F32, name="reserve_col")
+        fac_cols = sb.tile([P, PASSES, PACK], F32, name="fac_cols")
+        ground_sb = sb.tile([P, T], F32, name="ground_sb")
+        chunks = [(g, c) for g in range(PASSES) for c in range(OUT_TILES)]
+        v_raw = {gc: sb.tile([P, PACK, OUT_N], F32, name=f"v_raw{gc[0]}{gc[1]}") for gc in chunks}
+
+        nc.vector.memset(key_scales[:].bitcast(U32), 0)
+
+        words = keys_words[0].rearrange("p n t -> p (n t)")
+        nc.sync.dma_start(out=q_raw[:], in_=query.rearrange("(p j) q -> p j q", j=PACK))
+        nc.sync.dma_start(out=key_codes[0][:].bitcast(I32), in_=words[:, 0 : 4 * K_PASS].bitcast(I32))
+        for quad in range(4):
+            rows = keys_scales[0, 4 * quad : 4 * quad + 4, :].bitcast(I32)
+            nc.sync.dma_start(
+                out=key_scales[32 * quad : 32 * quad + 16, :].bitcast(I32),
+                in_=rows.rearrange("r (h c) -> h r c", h=SCORE_TILES),
+            )
+        nc.sync.dma_start(out=key_codes[1][:].bitcast(I32), in_=words[:, 4 * K_PASS : 8 * K_PASS].bitcast(I32))
+
+        def load_vals(gc):
+            g, c = gc
+            rows = vals[g * K_PASS : (g + 1) * K_PASS, c * OUT_N : (c + 1) * OUT_N]
+            nc.sync.dma_start(out=v_raw[gc][:], in_=rows.rearrange("(p j) e -> p j e", j=PACK))
+
+        load_vals(chunks[0])
+        nc.sync.dma_start(offsets[:], offs)
+        nc.sync.dma_start(out=th_col[:], in_=th)
+        load_vals(chunks[1])
+        nc.sync.dma_start(out=reserve_col[:], in_=reserve)
+        nc.sync.dma_start(out=fac_cols[:], in_=fac.rearrange("o (g p j) -> p (o g) j", g=PASSES, j=PACK))
+        nc.sync.dma_start(out=ground_sb[:], in_=ground)
+        load_vals(chunks[2])
+        load_vals(chunks[3])
+
+        ident = sb.tile([P, P], F32, name="ident")
+        make_identity(nc, ident[:])
+        placed = sb.tile([P, T], F32, name="placed")
+        nc.vector.memset(placed[:], 0.0)
+
+        q_bf = sb.tile([P, Q, PACK], BF16, name="q_bf", align_bytes=64)
+        q_codes = sb.tile([P, Q], U32, name="q_codes", align_bytes=64)
+        q_scales = sb.tile([P, Q], U8, name="q_scales", align_bytes=64)
+        nc.vector.tensor_copy(
+            out=q_bf[:].rearrange("p (c i) j -> p c j i", i=4),
+            in_=q_raw[:].rearrange("p j (c i) -> p c j i", i=4),
+        )
+        nc.vector.quantize_mx(
+            out=q_codes[:].bitcast(FP8X4), scales=q_scales[:], in_=q_bf[:].rearrange("p q j -> p (q j)")
+        )
+
+        scores = sb.tile([P, T], F32, name="scores")
+        for h in range(SCORE_TILES):
+            bank = psum.tile([P, SCORE_N], F32, name=f"score_bank{h}")
+            half, first = divmod(h * SCORE_N, K_PASS)
+            nc.tensor.matmul_mx(
+                out=bank[:],
+                lhsT=q_codes[:].bitcast(FP8X4),
+                lhsT_scale=q_scales[:],
+                rhs=key_codes[half][:, first : first + SCORE_N].bitcast(FP8X4),
+                rhs_scale=key_scales[4 * h : P, :],
+                start=True,
+                stop=True,
+            )
+            cols = scores[:, h * SCORE_N : (h + 1) * SCORE_N]
+            if h % 2 == 0:
+                nc.scalar.copy(out=cols, in_=bank[:])
+            else:
+                nc.vector.tensor_copy(out=cols, in_=bank[:])
+
+        neg_th = sb.tile([P, SLOTS], F32, name="neg_th")
+        nc.scalar.activation(neg_th[:], th_col[:].to_broadcast([P, SLOTS]), ACT.Copy, scale=-1.0)
+
+        v_bf = [sb.tile([P, E, PACK], BF16, name=f"v_bf{g}", align_bytes=64) for g in range(PASSES)]
+        v_codes = [sb.tile([P, E], U32, name=f"v_codes{g}", align_bytes=64) for g in range(PASSES)]
+
+        def round_vals(gc):
+            g, c = gc
+            nc.scalar.copy(
+                out=v_bf[g][:, c * OUT_N : (c + 1) * OUT_N, :].rearrange("p (c i) j -> p c j i", i=4),
+                in_=v_raw[gc][:].rearrange("p j (c i) -> p c j i", i=4),
+            )
+
+        def quantize_vals(g, scales, first, last):
+            nc.vector.quantize_mx(
+                out=v_codes[g][:, first:last].bitcast(FP8X4),
+                scales=scales,
+                in_=v_bf[g][:, first:last, :].rearrange("p e j -> p (e j)"),
+            )
+
+        listed = sb.tile([P, SLOTS], F32, name="listed")
+        nc.vector.tensor_copy(listed[:], scores[:].indirect(offsets[:]))
+        round_vals(chunks[0])
+        nc.vector.tensor_tensor(placed[:].indirect(offsets[:]), listed[:], neg_th[:], ALU.add)
+
+        passed = v_bf[0][:, OUT_N : OUT_N + SLOTS // PACK, :].rearrange("p e j -> p (e j)")
+        row_sum = sb.tile([P, 1], F32, name="row_sum")
+        denom = sb.tile([P, 1], F32, name="denom", tag="after_denom", align_bytes=64)
+        inv = sb.tile([P, 1], F32, name="inv")
+        nc.scalar.activation(passed, listed[:], ACT.Relu, bias=neg_th[:, 0:1], accum_out=row_sum[:])
+        nc.scalar.activation(denom[:], row_sum[:], ACT.Identity, bias=reserve_col[:])
+        for gc in chunks[1:]:
+            round_vals(gc)
+        nc.vector.reciprocal(inv[:], denom[:])
+
+        w_banks = [psum.tile([P, PACK, Q], F32, name=f"w_bank{g}") for g in range(PASSES)]
+        for g in range(PASSES):
+            for j in range(PACK):
+                nc.tensor.matmul(
+                    w_banks[g][:, j, :],
+                    lhsT=ground_sb[:, g * K_PASS + j : (g + 1) * K_PASS : PACK],
+                    rhs=ident[:],
+                    is_transpose=True,
+                    start=(j == 0),
+                    stop=False,
+                )
+
+        dealt = [sb.tile([P, PACK, P], F32, name=f"dealt{g}", tag=f"dealt{g}", align_bytes=64) for g in range(PASSES)]
+        for g in range(PASSES):
+            step = PACK // 2 if g == 0 else PACK
+            for j0 in range(0, PACK, step):
+                nc.vector.tensor_scalar(
+                    dealt[g][:, j0 : j0 + step, :].rearrange("q j p -> q p j"),
+                    placed[:, g * K_PASS : (g + 1) * K_PASS].rearrange("q (p j) -> q p j", j=PACK)[:, :, j0 : j0 + step],
+                    0.0,
+                    inv[:],
+                    ALU.max,
+                    ALU.mult,
+                )
+            for j in range(PACK):
+                nc.tensor.matmul(
+                    w_banks[g][:, j, :],
+                    lhsT=dealt[g][:, j, :],
+                    rhs=ident[:],
+                    is_transpose=True,
+                    start=False,
+                    stop=(j == PACK - 1),
+                )
+        first_scales = sb.tile([P, E], U8, name="first_scales", tag="after_denom", align_bytes=64)
+        quantize_vals(0, first_scales[:], 0, E)
+        v_scales = {(0, c): first_scales[:, c * OUT_N : (c + 1) * OUT_N] for c in range(OUT_TILES)}
+
+        w_bf = [sb.tile([P, Q, PACK], BF16, name=f"w_bf{g}", align_bytes=64) for g in range(PASSES)]
+        w_codes = [sb.tile([P, Q], U32, name=f"w_codes{g}", align_bytes=64) for g in range(PASSES)]
+        w_scales = [sb.tile([P, Q], U8, name=f"w_scales{g}", align_bytes=64) for g in range(PASSES)]
+        for g in range(PASSES):
+            nc.vector.tensor_tensor(
+                w_bf[g][:],
+                w_banks[g][:].rearrange("p j q -> p q j"),
+                fac_cols[:, g : g + 1, :].to_broadcast([P, Q, PACK]),
+                ALU.mult,
+            )
+            late_scales = sb.tile([P, OUT_N], U8, name=f"late_scales{g}", tag=f"dealt{g}", align_bytes=64)
+            v_scales[1, g] = late_scales[:]
+            quantize_vals(1, late_scales[:], g * OUT_N, (g + 1) * OUT_N)
+            nc.vector.quantize_mx(
+                out=w_codes[g][:].bitcast(FP8X4), scales=w_scales[g][:], in_=w_bf[g][:].rearrange("p q j -> p (q j)")
+            )
+
+        out_banks = [psum.tile([P, OUT_N], F32, name=f"out_bank{c}") for c in range(OUT_TILES)]
+        for g, c in chunks:
+            nc.tensor.matmul_mx(
+                out=out_banks[c][:],
+                lhsT=w_codes[g][:].bitcast(FP8X4),
+                lhsT_scale=w_scales[g][:],
+                rhs=v_codes[g][:, c * OUT_N : (c + 1) * OUT_N].bitcast(FP8X4),
+                rhs_scale=v_scales[g, c],
+                start=(g == 0),
+                stop=(g == PASSES - 1),
+            )
+        result = [sb.tile([P, OUT_N], F32, name=f"result{c}") for c in range(OUT_TILES)]
+        nc.scalar.copy(out=result[0][:], in_=out_banks[0][:])
+        nc.scalar.dma_start(out=out[:, 0:OUT_N], in_=result[0][:])
+        nc.vector.tensor_copy(out=result[1][:], in_=out_banks[1][:])
+        nc.sync.dma_start(out=out[:, OUT_N : 2 * OUT_N], in_=result[1][:])

@@ -34,11 +34,11 @@ def tile_attend_spotlight_heads_kernel(tc, query, keys_words, keys_scales, th, r
 
         offsets = sb.tile([P, SLOTS // 16], U16, name="offsets")
         q_raw = sb.tile([P, PACK, Q], F32, name="q_raw")
-        key_codes = [sb.tile([P, K_PASS], U32, name=f"key_codes{h}", align_bytes=64) for h in range(2)]
+        key_codes = [sb.tile([P, K_PASS], U32, name=f"key_codes{h}", tag=f"key_codes{h}", align_bytes=64) for h in range(2)]
         key_scales = sb.tile([P, SCORE_N], U8, name="key_scales", align_bytes=64)
         th_col = sb.tile([P, 1], F32, name="th_col")
         reserve_col = sb.tile([P, 1], F32, name="reserve_col")
-        fac_cols = sb.tile([P, PASSES, PACK], F32, name="fac_cols")
+        fac_cols = sb.tile([P, PASSES, PACK], F32, name="fac_cols", tag="after_weights", align_bytes=64)
         ground_sb = sb.tile([P, T], F32, name="ground_sb")
         chunks = [(g, c) for g in range(PASSES) for c in range(OUT_TILES)]
         v_raw = {gc: sb.tile([P, PACK, OUT_N], F32, name=f"v_raw{gc[0]}{gc[1]}") for gc in chunks}
@@ -64,10 +64,10 @@ def tile_attend_spotlight_heads_kernel(tc, query, keys_words, keys_scales, th, r
         load_vals(chunks[0])
         nc.sync.dma_start(offsets[:], offs)
         nc.sync.dma_start(out=th_col[:], in_=th)
-        load_vals(chunks[1])
+        nc.sync.dma_start(out=ground_sb[:], in_=ground)
         nc.sync.dma_start(out=reserve_col[:], in_=reserve)
         nc.sync.dma_start(out=fac_cols[:], in_=fac.rearrange("o (g p j) -> p (o g) j", g=PASSES, j=PACK))
-        nc.sync.dma_start(out=ground_sb[:], in_=ground)
+        load_vals(chunks[1])
         load_vals(chunks[2])
         load_vals(chunks[3])
 
@@ -78,38 +78,44 @@ def tile_attend_spotlight_heads_kernel(tc, query, keys_words, keys_scales, th, r
 
         q_bf = sb.tile([P, Q, PACK], BF16, name="q_bf", align_bytes=64)
         q_codes = sb.tile([P, Q], U32, name="q_codes", align_bytes=64)
-        q_scales = sb.tile([P, Q], U8, name="q_scales", align_bytes=64)
-        nc.vector.tensor_copy(
-            out=q_bf[:].rearrange("p (c i) j -> p c j i", i=4),
-            in_=q_raw[:].rearrange("p j (c i) -> p c j i", i=4),
-        )
-        nc.vector.quantize_mx(
-            out=q_codes[:].bitcast(FP8X4), scales=q_scales[:], in_=q_bf[:].rearrange("p q j -> p (q j)")
-        )
+        q_scales = sb.tile([P, Q], U8, name="q_scales", tag="after_scores", align_bytes=64)
+        halves = [slice(0, Q // 2), slice(Q // 2, Q)]
+        for half in halves:
+            nc.vector.tensor_copy(
+                out=q_bf[:, half, :].rearrange("p (c i) j -> p c j i", i=4),
+                in_=q_raw[:, :, half].rearrange("p j (c i) -> p c j i", i=4),
+            )
+        for half in halves:
+            nc.vector.quantize_mx(
+                out=q_codes[:, half].bitcast(FP8X4),
+                scales=q_scales[:, half],
+                in_=q_bf[:, half, :].rearrange("p q j -> p (q j)"),
+            )
 
         scores = sb.tile([P, T], F32, name="scores")
-        for h in range(SCORE_TILES):
-            bank = psum.tile([P, SCORE_N], F32, name=f"score_bank{h}")
-            half, first = divmod(h * SCORE_N, K_PASS)
+        score_cuts = [0, 256, 512, 768, 896, 1024]
+        for n, (first, last) in enumerate(zip(score_cuts, score_cuts[1:])):
+            bank = psum.tile([P, last - first], F32, name=f"score_bank{n}", tag=f"bank{n}")
+            plane, col = divmod(first, SCORE_N)
+            half, word = divmod(first, K_PASS)
             nc.tensor.matmul_mx(
                 out=bank[:],
                 lhsT=q_codes[:].bitcast(FP8X4),
                 lhsT_scale=q_scales[:],
-                rhs=key_codes[half][:, first : first + SCORE_N].bitcast(FP8X4),
-                rhs_scale=key_scales[4 * h : P, :],
+                rhs=key_codes[half][:, word : word + last - first].bitcast(FP8X4),
+                rhs_scale=key_scales[4 * plane : P, col : col + last - first],
                 start=True,
                 stop=True,
             )
-            cols = scores[:, h * SCORE_N : (h + 1) * SCORE_N]
-            if h % 2 == 0:
-                nc.scalar.copy(out=cols, in_=bank[:])
+            if n % 2 == 1:
+                nc.scalar.copy(out=scores[:, first:last], in_=bank[:])
             else:
-                nc.vector.tensor_copy(out=cols, in_=bank[:])
+                nc.vector.tensor_copy(out=scores[:, first:last], in_=bank[:])
 
-        neg_th = sb.tile([P, SLOTS], F32, name="neg_th")
+        neg_th = sb.tile([P, SLOTS], F32, name="neg_th", tag="after_scores", align_bytes=64)
         nc.scalar.activation(neg_th[:], th_col[:].to_broadcast([P, SLOTS]), ACT.Copy, scale=-1.0)
 
-        v_bf = [sb.tile([P, E, PACK], BF16, name=f"v_bf{g}", align_bytes=64) for g in range(PASSES)]
+        v_bf = [sb.tile([P, E, PACK], BF16, name=f"v_bf{g}", tag=f"key_codes{1 - g}", align_bytes=64) for g in range(PASSES)]
         v_codes = [sb.tile([P, E], U32, name=f"v_codes{g}", align_bytes=64) for g in range(PASSES)]
 
         def round_vals(gc):
@@ -132,7 +138,7 @@ def tile_attend_spotlight_heads_kernel(tc, query, keys_words, keys_scales, th, r
         nc.vector.tensor_tensor(placed[:].indirect(offsets[:]), listed[:], neg_th[:], ALU.add)
 
         passed = v_bf[0][:, OUT_N : OUT_N + SLOTS // PACK, :].rearrange("p e j -> p (e j)")
-        row_sum = sb.tile([P, 1], F32, name="row_sum")
+        row_sum = sb.tile([P, 1], F32, name="row_sum", tag="after_sum", align_bytes=64)
         denom = sb.tile([P, 1], F32, name="denom", tag="after_denom", align_bytes=64)
         inv = sb.tile([P, 1], F32, name="inv")
         nc.scalar.activation(passed, listed[:], ACT.Relu, bias=neg_th[:, 0:1], accum_out=row_sum[:])
@@ -140,6 +146,8 @@ def tile_attend_spotlight_heads_kernel(tc, query, keys_words, keys_scales, th, r
         for gc in chunks[1:]:
             round_vals(gc)
         nc.vector.reciprocal(inv[:], denom[:])
+        first_scales = sb.tile([P, OUT_N], U8, name="first_scales", tag="after_sum", align_bytes=64)
+        quantize_vals(0, first_scales[:], 0, OUT_N)
 
         w_banks = [psum.tile([P, PACK, Q], F32, name=f"w_bank{g}") for g in range(PASSES)]
         for g in range(PASSES):
@@ -174,40 +182,66 @@ def tile_attend_spotlight_heads_kernel(tc, query, keys_words, keys_scales, th, r
                     start=False,
                     stop=(j == PACK - 1),
                 )
-        first_scales = sb.tile([P, E], U8, name="first_scales", tag="after_denom", align_bytes=64)
-        quantize_vals(0, first_scales[:], 0, E)
-        v_scales = {(0, c): first_scales[:, c * OUT_N : (c + 1) * OUT_N] for c in range(OUT_TILES)}
+        mid_scales = sb.tile([P, 2 * OUT_N], U8, name="mid_scales", tag="after_denom", align_bytes=64)
+        quantize_vals(0, mid_scales[:, 0:OUT_N], OUT_N, E)
+        quantize_vals(1, mid_scales[:, OUT_N : 2 * OUT_N], 0, OUT_N)
 
-        w_bf = [sb.tile([P, Q, PACK], BF16, name=f"w_bf{g}", align_bytes=64) for g in range(PASSES)]
+        w_bf = [sb.tile([P, Q, PACK], BF16, name=f"w_bf{g}", tag=f"w_bf{g}", align_bytes=64) for g in range(PASSES)]
         w_codes = [sb.tile([P, Q], U32, name=f"w_codes{g}", align_bytes=64) for g in range(PASSES)]
-        w_scales = [sb.tile([P, Q], U8, name=f"w_scales{g}", align_bytes=64) for g in range(PASSES)]
-        for g in range(PASSES):
+        w_scales = [
+            sb.tile([P, Q], U8, name=f"w_scales{g}", tag=f"dealt{1 - g}", align_bytes=64) for g in range(PASSES)
+        ]
+
+        def weigh(g, cols):
             nc.vector.tensor_tensor(
-                w_bf[g][:],
-                w_banks[g][:].rearrange("p j q -> p q j"),
-                fac_cols[:, g : g + 1, :].to_broadcast([P, Q, PACK]),
+                w_bf[g][:, cols, :],
+                w_banks[g][:, :, cols].rearrange("p j q -> p q j"),
+                fac_cols[:, g : g + 1, :].to_broadcast([P, cols.stop - cols.start, PACK]),
                 ALU.mult,
             )
-            late_scales = sb.tile([P, OUT_N], U8, name=f"late_scales{g}", tag=f"dealt{g}", align_bytes=64)
-            v_scales[1, g] = late_scales[:]
-            quantize_vals(1, late_scales[:], g * OUT_N, (g + 1) * OUT_N)
+
+        def quantize_weights(g, cols):
             nc.vector.quantize_mx(
-                out=w_codes[g][:].bitcast(FP8X4), scales=w_scales[g][:], in_=w_bf[g][:].rearrange("p q j -> p (q j)")
+                out=w_codes[g][:, cols].bitcast(FP8X4),
+                scales=w_scales[g][:, cols],
+                in_=w_bf[g][:, cols, :].rearrange("p q j -> p (q j)"),
             )
 
-        out_banks = [psum.tile([P, OUT_N], F32, name=f"out_bank{c}") for c in range(OUT_TILES)]
-        for g, c in chunks:
-            nc.tensor.matmul_mx(
-                out=out_banks[c][:],
-                lhsT=w_codes[g][:].bitcast(FP8X4),
-                lhsT_scale=w_scales[g][:],
-                rhs=v_codes[g][:, c * OUT_N : (c + 1) * OUT_N].bitcast(FP8X4),
-                rhs_scale=v_scales[g, c],
-                start=(g == 0),
-                stop=(g == PASSES - 1),
-            )
+        weigh(0, slice(0, Q))
+        weigh(1, halves[0])
+        quantize_weights(0, slice(0, Q))
+        weigh(1, halves[1])
+        quantize_weights(1, halves[0])
+        quantize_weights(1, halves[1])
+        last_scales = sb.tile([P, OUT_N], U8, name="last_scales", tag="after_weights", align_bytes=64)
+        quantize_vals(1, last_scales[:], OUT_N, E)
+        v_scales = {
+            (0, 0): first_scales[:],
+            (0, 1): mid_scales[:, 0:OUT_N],
+            (1, 0): mid_scales[:, OUT_N : 2 * OUT_N],
+            (1, 1): last_scales[:],
+        }
+
+        out_cuts = [0, 256, 384, 512]
+        spans = list(zip(out_cuts, out_cuts[1:]))
+        out_banks = [
+            psum.tile([P, last - first], F32, name=f"out_bank{n}", tag=f"bank{n}") for n, (first, last) in enumerate(spans)
+        ]
+        for g in range(PASSES):
+            for n, (first, last) in enumerate(spans):
+                c, col = divmod(first, OUT_N)
+                nc.tensor.matmul_mx(
+                    out=out_banks[n][:],
+                    lhsT=w_codes[g][:].bitcast(FP8X4),
+                    lhsT_scale=w_scales[g][:],
+                    rhs=v_codes[g][:, first:last].bitcast(FP8X4),
+                    rhs_scale=v_scales[g, c][:, col : col + last - first],
+                    start=(g == 0),
+                    stop=(g == PASSES - 1),
+                )
         result = [sb.tile([P, OUT_N], F32, name=f"result{c}") for c in range(OUT_TILES)]
         nc.scalar.copy(out=result[0][:], in_=out_banks[0][:])
         nc.scalar.dma_start(out=out[:, 0:OUT_N], in_=result[0][:])
-        nc.vector.tensor_copy(out=result[1][:], in_=out_banks[1][:])
+        nc.vector.tensor_copy(out=result[1][:, 0:128], in_=out_banks[1][:])
+        nc.vector.tensor_copy(out=result[1][:, 128:256], in_=out_banks[2][:])
         nc.sync.dma_start(out=out[:, OUT_N : 2 * OUT_N], in_=result[1][:])

@@ -38,7 +38,7 @@ def tile_attend_spotlight_heads_kernel(tc, query, keys_words, keys_scales, th, r
         key_scales = sb.tile([P, SCORE_N], U8, name="key_scales", align_bytes=64)
         th_col = sb.tile([P, 1], F32, name="th_col")
         reserve_col = sb.tile([P, 1], F32, name="reserve_col")
-        fac_cols = sb.tile([P, PASSES, PACK], F32, name="fac_cols", tag="after_weights", align_bytes=64)
+        fac_cols = sb.tile([P, PASSES, PACK], F32, name="fac_cols")
         ground_sb = sb.tile([P, T], F32, name="ground_sb")
         chunks = [(g, c) for g in range(PASSES) for c in range(OUT_TILES)]
         v_raw = {gc: sb.tile([P, PACK, OUT_N], F32, name=f"v_raw{gc[0]}{gc[1]}") for gc in chunks}
@@ -63,16 +63,16 @@ def tile_attend_spotlight_heads_kernel(tc, query, keys_words, keys_scales, th, r
 
         load_vals(chunks[0])
         nc.sync.dma_start(offsets[:], offs)
-        nc.sync.dma_start(out=th_col[:], in_=th)
         nc.sync.dma_start(out=ground_sb[:], in_=ground)
         nc.sync.dma_start(out=reserve_col[:], in_=reserve)
-        nc.sync.dma_start(out=fac_cols[:], in_=fac.rearrange("o (g p j) -> p (o g) j", g=PASSES, j=PACK))
         load_vals(chunks[1])
         load_vals(chunks[2])
         load_vals(chunks[3])
+        nc.sync.dma_start(out=fac_cols[:], in_=fac.rearrange("o (g p j) -> p (o g) j", g=PASSES, j=PACK))
 
         ident = sb.tile([P, P], F32, name="ident")
         make_identity(nc, ident[:])
+        nc.gpsimd.dma_start(out=th_col[:], in_=th)
         placed = sb.tile([P, T], F32, name="placed")
         nc.vector.memset(placed[:], 0.0)
 
@@ -80,8 +80,8 @@ def tile_attend_spotlight_heads_kernel(tc, query, keys_words, keys_scales, th, r
         q_codes = sb.tile([P, Q], U32, name="q_codes", align_bytes=64)
         q_scales = sb.tile([P, Q], U8, name="q_scales", tag="after_scores", align_bytes=64)
         halves = [slice(0, Q // 2), slice(Q // 2, Q)]
-        for half in halves:
-            nc.vector.tensor_copy(
+        for half, copy in zip(halves, (nc.vector.tensor_copy, nc.scalar.copy)):
+            copy(
                 out=q_bf[:, half, :].rearrange("p (c i) j -> p c j i", i=4),
                 in_=q_raw[:, :, half].rearrange("p j (c i) -> p c j i", i=4),
             )
@@ -113,7 +113,7 @@ def tile_attend_spotlight_heads_kernel(tc, query, keys_words, keys_scales, th, r
                 nc.vector.tensor_copy(out=scores[:, first:last], in_=bank[:])
 
         neg_th = sb.tile([P, SLOTS], F32, name="neg_th", tag="after_scores", align_bytes=64)
-        nc.scalar.activation(neg_th[:], th_col[:].to_broadcast([P, SLOTS]), ACT.Copy, scale=-1.0)
+        nc.vector.tensor_scalar(neg_th[:], th_col[:].to_broadcast([P, SLOTS]), -1.0, None, ALU.mult)
 
         v_bf = [sb.tile([P, E, PACK], BF16, name=f"v_bf{g}", tag=f"key_codes{1 - g}", align_bytes=64) for g in range(PASSES)]
         v_codes = [sb.tile([P, E], U32, name=f"v_codes{g}", align_bytes=64) for g in range(PASSES)]
@@ -149,15 +149,18 @@ def tile_attend_spotlight_heads_kernel(tc, query, keys_words, keys_scales, th, r
         first_scales = sb.tile([P, OUT_N], U8, name="first_scales", tag="after_sum", align_bytes=64)
         quantize_vals(0, first_scales[:], 0, OUT_N)
 
-        w_banks = [psum.tile([P, PACK, Q], F32, name=f"w_bank{g}") for g in range(PASSES)]
+        first_bank = psum.tile([P, PACK, Q], F32, name="first_bank", tag="bank5")
+        turned = {(0, j): first_bank[:, j, :] for j in range(PACK)}
+        for j in range(PACK):
+            turned[1, j] = psum.tile([P, Q], F32, name=f"second_bank{j}", tag=f"bank{j}")[:]
         for g in range(PASSES):
             for j in range(PACK):
                 nc.tensor.matmul(
-                    w_banks[g][:, j, :],
+                    turned[g, j],
                     lhsT=ground_sb[:, g * K_PASS + j : (g + 1) * K_PASS : PACK],
                     rhs=ident[:],
                     is_transpose=True,
-                    start=(j == 0),
+                    start=(g == 1 or j == 0),
                     stop=False,
                 )
 
@@ -175,12 +178,12 @@ def tile_attend_spotlight_heads_kernel(tc, query, keys_words, keys_scales, th, r
                 )
             for j in range(PACK):
                 nc.tensor.matmul(
-                    w_banks[g][:, j, :],
+                    turned[g, j],
                     lhsT=dealt[g][:, j, :],
                     rhs=ident[:],
                     is_transpose=True,
                     start=False,
-                    stop=(j == PACK - 1),
+                    stop=(g == 1 or j == PACK - 1),
                 )
         mid_scales = sb.tile([P, 2 * OUT_N], U8, name="mid_scales", tag="after_denom", align_bytes=64)
         quantize_vals(0, mid_scales[:, 0:OUT_N], OUT_N, E)
@@ -188,17 +191,7 @@ def tile_attend_spotlight_heads_kernel(tc, query, keys_words, keys_scales, th, r
 
         w_bf = [sb.tile([P, Q, PACK], BF16, name=f"w_bf{g}", tag=f"w_bf{g}", align_bytes=64) for g in range(PASSES)]
         w_codes = [sb.tile([P, Q], U32, name=f"w_codes{g}", align_bytes=64) for g in range(PASSES)]
-        w_scales = [
-            sb.tile([P, Q], U8, name=f"w_scales{g}", tag=f"dealt{1 - g}", align_bytes=64) for g in range(PASSES)
-        ]
-
-        def weigh(g, cols):
-            nc.vector.tensor_tensor(
-                w_bf[g][:, cols, :],
-                w_banks[g][:, :, cols].rearrange("p j q -> p q j"),
-                fac_cols[:, g : g + 1, :].to_broadcast([P, cols.stop - cols.start, PACK]),
-                ALU.mult,
-            )
+        w_scales = [sb.tile([P, Q], U8, name=f"w_scales{g}", align_bytes=64) for g in range(PASSES)]
 
         def quantize_weights(g, cols):
             nc.vector.quantize_mx(
@@ -207,14 +200,25 @@ def tile_attend_spotlight_heads_kernel(tc, query, keys_words, keys_scales, th, r
                 in_=w_bf[g][:, cols, :].rearrange("p q j -> p (q j)"),
             )
 
-        weigh(0, slice(0, Q))
-        weigh(1, halves[0])
-        quantize_weights(0, slice(0, Q))
-        weigh(1, halves[1])
-        quantize_weights(1, halves[0])
-        quantize_weights(1, halves[1])
-        last_scales = sb.tile([P, OUT_N], U8, name="last_scales", tag="after_weights", align_bytes=64)
+        nc.vector.tensor_tensor(
+            w_bf[0][:],
+            first_bank[:].rearrange("p j q -> p q j"),
+            fac_cols[:, 0:1, :].to_broadcast([P, Q, PACK]),
+            ALU.mult,
+        )
+        last_scales = sb.tile([P, OUT_N], U8, name="last_scales", tag="dealt0", align_bytes=64)
         quantize_vals(1, last_scales[:], OUT_N, E)
+        quantize_weights(0, slice(0, Q))
+        w_rows = sb.tile([P, PACK, Q], BF16, name="w_rows")
+        for j in range(PACK):
+            nc.scalar.activation(w_rows[:, j, :], turned[1, j], ACT.Copy, scale=fac_cols[:, 1, j : j + 1])
+        for half in halves:
+            nc.vector.tensor_copy(
+                out=w_bf[1][:, half, :].rearrange("p (c i) j -> p c j i", i=4),
+                in_=w_rows[:, :, half].rearrange("p j (c i) -> p c j i", i=4),
+            )
+        for half in halves:
+            quantize_weights(1, half)
         v_scales = {
             (0, 0): first_scales[:],
             (0, 1): mid_scales[:, 0:OUT_N],
@@ -225,7 +229,7 @@ def tile_attend_spotlight_heads_kernel(tc, query, keys_words, keys_scales, th, r
         out_cuts = [0, 256, 384, 512]
         spans = list(zip(out_cuts, out_cuts[1:]))
         out_banks = [
-            psum.tile([P, last - first], F32, name=f"out_bank{n}", tag=f"bank{n}") for n, (first, last) in enumerate(spans)
+            psum.tile([P, last - first], F32, name=f"out_bank{n}", tag=f"bank{(4, 6, 7)[n]}") for n, (first, last) in enumerate(spans)
         ]
         for g in range(PASSES):
             for n, (first, last) in enumerate(spans):
@@ -239,9 +243,10 @@ def tile_attend_spotlight_heads_kernel(tc, query, keys_words, keys_scales, th, r
                     start=(g == 0),
                     stop=(g == PASSES - 1),
                 )
-        result = [sb.tile([P, OUT_N], F32, name=f"result{c}") for c in range(OUT_TILES)]
+        result = [sb.tile([P, last - first], F32, name=f"result{n}") for n, (first, last) in enumerate(spans)]
         nc.scalar.copy(out=result[0][:], in_=out_banks[0][:])
-        nc.scalar.dma_start(out=out[:, 0:OUT_N], in_=result[0][:])
-        nc.vector.tensor_copy(out=result[1][:, 0:128], in_=out_banks[1][:])
-        nc.vector.tensor_copy(out=result[1][:, 128:256], in_=out_banks[2][:])
-        nc.sync.dma_start(out=out[:, OUT_N : 2 * OUT_N], in_=result[1][:])
+        nc.scalar.dma_start(out=out[:, 0:256], in_=result[0][:])
+        nc.vector.tensor_copy(out=result[1][:], in_=out_banks[1][:])
+        nc.sync.dma_start(out=out[:, 256:384], in_=result[1][:])
+        nc.vector.tensor_copy(out=result[2][:], in_=out_banks[2][:])
+        nc.sync.dma_start(out=out[:, 384:512], in_=result[2][:])

@@ -61,18 +61,18 @@ def tile_attend_spotlight_heads_kernel(tc, query, keys_words, keys_scales, th, r
             rows = vals[g * K_PASS : (g + 1) * K_PASS, c * OUT_N : (c + 1) * OUT_N]
             nc.sync.dma_start(out=v_raw[gc][:], in_=rows.rearrange("(p j) e -> p j e", j=PACK))
 
-        load_vals(chunks[0])
-        nc.sync.dma_start(offsets[:], offs)
         nc.sync.dma_start(out=ground_sb[:], in_=ground)
-        nc.sync.dma_start(out=reserve_col[:], in_=reserve)
+        nc.sync.dma_start(offsets[:], offs)
+        nc.sync.dma_start(out=th_col[:], in_=th)
+        load_vals(chunks[0])
         load_vals(chunks[1])
+        nc.sync.dma_start(out=reserve_col[:], in_=reserve)
         load_vals(chunks[2])
         load_vals(chunks[3])
         nc.sync.dma_start(out=fac_cols[:], in_=fac.rearrange("o (g p j) -> p (o g) j", g=PASSES, j=PACK))
 
         ident = sb.tile([P, P], F32, name="ident")
         make_identity(nc, ident[:])
-        nc.gpsimd.dma_start(out=th_col[:], in_=th)
         placed = sb.tile([P, T], F32, name="placed")
         nc.vector.memset(placed[:], 0.0)
 
@@ -209,13 +209,14 @@ def tile_attend_spotlight_heads_kernel(tc, query, keys_words, keys_scales, th, r
         last_scales = sb.tile([P, OUT_N], U8, name="last_scales", tag="dealt0", align_bytes=64)
         quantize_vals(1, last_scales[:], OUT_N, E)
         quantize_weights(0, slice(0, Q))
-        w_rows = sb.tile([P, PACK, Q], BF16, name="w_rows")
+        w_pairs = sb.tile([P, PACK // 2, Q, 2], BF16, name="w_pairs")
         for j in range(PACK):
-            nc.scalar.activation(w_rows[:, j, :], turned[1, j], ACT.Copy, scale=fac_cols[:, 1, j : j + 1])
+            nc.scalar.activation(w_pairs[:, j // 2, :, j % 2], turned[1, j], ACT.Copy, scale=fac_cols[:, 1, j : j + 1])
+        pair_words = w_pairs[:].rearrange("p u q e -> p u (q e)").bitcast(F32)
         for half in halves:
             nc.vector.tensor_copy(
-                out=w_bf[1][:, half, :].rearrange("p (c i) j -> p c j i", i=4),
-                in_=w_rows[:, :, half].rearrange("p j (c i) -> p c j i", i=4),
+                out=w_bf[1][:, half, :].bitcast(F32).rearrange("p (c i) u -> p c u i", i=4),
+                in_=pair_words[:, :, half].rearrange("p u (c i) -> p c u i", i=4),
             )
         for half in halves:
             quantize_weights(1, half)

@@ -107,7 +107,7 @@ def tile_attend_spotlight_heads_kernel(tc, query, keys_words, keys_scales, th, r
                 start=True,
                 stop=True,
             )
-            if n % 2 == 1:
+            if n % 2 == 0:
                 nc.scalar.copy(out=scores[:, first:last], in_=bank[:])
             else:
                 nc.vector.tensor_copy(out=scores[:, first:last], in_=bank[:])
@@ -138,7 +138,7 @@ def tile_attend_spotlight_heads_kernel(tc, query, keys_words, keys_scales, th, r
         nc.vector.tensor_tensor(placed[:].indirect(offsets[:]), listed[:], neg_th[:], ALU.add)
 
         passed = v_bf[0][:, OUT_N : OUT_N + SLOTS // PACK, :].rearrange("p e j -> p (e j)")
-        row_sum = sb.tile([P, 1], F32, name="row_sum", tag="after_sum", align_bytes=64)
+        row_sum = sb.tile([P, 1], F32, name="row_sum")
         denom = sb.tile([P, 1], F32, name="denom", tag="after_denom", align_bytes=64)
         inv = sb.tile([P, 1], F32, name="inv")
         nc.scalar.activation(passed, listed[:], ACT.Relu, bias=neg_th[:, 0:1], accum_out=row_sum[:])
@@ -146,8 +146,6 @@ def tile_attend_spotlight_heads_kernel(tc, query, keys_words, keys_scales, th, r
         for gc in chunks[1:]:
             round_vals(gc)
         nc.vector.reciprocal(inv[:], denom[:])
-        first_scales = sb.tile([P, OUT_N], U8, name="first_scales", tag="after_sum", align_bytes=64)
-        quantize_vals(0, first_scales[:], 0, OUT_N)
 
         first_bank = psum.tile([P, PACK, Q], F32, name="first_bank", tag="bank5")
         turned = {(0, j): first_bank[:, j, :] for j in range(PACK)}
@@ -185,9 +183,9 @@ def tile_attend_spotlight_heads_kernel(tc, query, keys_words, keys_scales, th, r
                     start=False,
                     stop=(g == 1 or j == PACK - 1),
                 )
-        mid_scales = sb.tile([P, 2 * OUT_N], U8, name="mid_scales", tag="after_denom", align_bytes=64)
-        quantize_vals(0, mid_scales[:, 0:OUT_N], OUT_N, E)
-        quantize_vals(1, mid_scales[:, OUT_N : 2 * OUT_N], 0, OUT_N)
+        mid_scales = sb.tile([P, 3 * OUT_N], U8, name="mid_scales", tag="after_denom", align_bytes=64)
+        quantize_vals(0, mid_scales[:, 0:E], 0, E)
+        quantize_vals(1, mid_scales[:, E : E + OUT_N], 0, OUT_N)
 
         w_bf = [sb.tile([P, Q, PACK], BF16, name=f"w_bf{g}", tag=f"w_bf{g}", align_bytes=64) for g in range(PASSES)]
         w_codes = [sb.tile([P, Q], U32, name=f"w_codes{g}", align_bytes=64) for g in range(PASSES)]
@@ -221,9 +219,9 @@ def tile_attend_spotlight_heads_kernel(tc, query, keys_words, keys_scales, th, r
         for half in halves:
             quantize_weights(1, half)
         v_scales = {
-            (0, 0): first_scales[:],
-            (0, 1): mid_scales[:, 0:OUT_N],
-            (1, 0): mid_scales[:, OUT_N : 2 * OUT_N],
+            (0, 0): mid_scales[:, 0:OUT_N],
+            (0, 1): mid_scales[:, OUT_N:E],
+            (1, 0): mid_scales[:, E : E + OUT_N],
             (1, 1): last_scales[:],
         }
 

from contextlib import ExitStack

import concourse.mybir as mybir
from concourse.masks import make_identity

D, E, T, Q, SLOTS = 512, 512, 1024, 128, 512
FLOPS = 2 * Q * D * T + 2 * Q * T * E

F32 = mybir.dt.float32
BF16 = mybir.dt.bfloat16
I32 = mybir.dt.int32
U32 = mybir.dt.uint32
U16 = mybir.dt.uint16
U8 = mybir.dt.uint8
FP8X4 = mybir.dt.float8_e4m3fn_x4
ALU = mybir.AluOpType
ACT = mybir.ActivationFunctionType

P = 128
PACK = 4
K_PASS = P * PACK
PASSES = T // K_PASS
SCORE_N = 256
SCORE_TILES = T // SCORE_N
OUT_N = 256
OUT_TILES = E // OUT_N


def tile_attend_spotlight_heads_kernel(tc, query, keys_words, keys_scales, th, reserve, ground, fac, vals, offs, out):
    nc = tc.nc
    with ExitStack() as ctx:
        sb = ctx.enter_context(tc.tile_pool(name="sb", bufs=1))
        psum = ctx.enter_context(tc.psum_pool(name="psum", bufs=1))

        offsets = sb.tile([P, SLOTS // 16], U16, name="offsets")
        q_raw = sb.tile([P, PACK, Q], F32, name="q_raw")
        key_codes = [sb.tile([P, K_PASS], U32, name=f"key_codes{h}", tag=f"key_codes{h}", align_bytes=64) for h in range(2)]
        key_scales = sb.tile([P, SCORE_N], U8, name="key_scales", align_bytes=64)
        th_col = sb.tile([P, 1], F32, name="th_col")
        reserve_col = sb.tile([P, 1], F32, name="reserve_col")
        fac_cols = sb.tile([P, PASSES, PACK], F32, name="fac_cols")
        ground_sb = sb.tile([P, T], F32, name="ground_sb")
        chunks = [(g, c) for g in range(PASSES) for c in range(OUT_TILES)]
        v_raw = {gc: sb.tile([P, PACK, OUT_N], F32, name=f"v_raw{gc[0]}{gc[1]}") for gc in chunks}

        nc.vector.memset(key_scales[:].bitcast(U32), 0)

        words = keys_words[0].rearrange("p n t -> p (n t)")
        nc.sync.dma_start(out=q_raw[:], in_=query.rearrange("(p j) q -> p j q", j=PACK))
        nc.sync.dma_start(out=key_codes[0][:].bitcast(I32), in_=words[:, 0 : 4 * K_PASS].bitcast(I32))
        for quad in range(4):
            rows = keys_scales[0, 4 * quad : 4 * quad + 4, :].bitcast(I32)
            nc.sync.dma_start(
                out=key_scales[32 * quad : 32 * quad + 16, :].bitcast(I32),
                in_=rows.rearrange("r (h c) -> h r c", h=SCORE_TILES),
            )
        nc.sync.dma_start(out=key_codes[1][:].bitcast(I32), in_=words[:, 4 * K_PASS : 8 * K_PASS].bitcast(I32))

        def load_vals(gc):
            g, c = gc
            rows = vals[g * K_PASS : (g + 1) * K_PASS, c * OUT_N : (c + 1) * OUT_N]
            nc.sync.dma_start(out=v_raw[gc][:], in_=rows.rearrange("(p j) e -> p j e", j=PACK))

        nc.sync.dma_start(out=ground_sb[:], in_=ground)
        nc.sync.dma_start(offsets[:], offs)
        nc.sync.dma_start(out=th_col[:], in_=th)
        load_vals(chunks[0])
        load_vals(chunks[1])
        nc.sync.dma_start(out=reserve_col[:], in_=reserve)
        load_vals(chunks[2])
        load_vals(chunks[3])
        nc.sync.dma_start(out=fac_cols[:], in_=fac.rearrange("o (g p j) -> p (o g) j", g=PASSES, j=PACK))

        ident = sb.tile([P, P], F32, name="ident")
        make_identity(nc, ident[:])
        placed = sb.tile([P, T], F32, name="placed")
        nc.vector.memset(placed[:], 0.0)

        q_bf = sb.tile([P, Q, PACK], BF16, name="q_bf", align_bytes=64)
        q_codes = sb.tile([P, Q], U32, name="q_codes", align_bytes=64)
        q_scales = sb.tile([P, Q], U8, name="q_scales", tag="after_scores", align_bytes=64)
        halves = [slice(0, Q // 2), slice(Q // 2, Q)]
        for half, copy in zip(halves, (nc.vector.tensor_copy, nc.scalar.copy)):
            copy(
                out=q_bf[:, half, :].rearrange("p (c i) j -> p c j i", i=4),
                in_=q_raw[:, :, half].rearrange("p j (c i) -> p c j i", i=4),
            )
        for half in halves:
            nc.vector.quantize_mx(
                out=q_codes[:, half].bitcast(FP8X4),
                scales=q_scales[:, half],
                in_=q_bf[:, half, :].rearrange("p q j -> p (q j)"),
            )

        scores = sb.tile([P, T], F32, name="scores")
        score_cuts = [0, 256, 512, 768, 896, 1024]
        for n, (first, last) in enumerate(zip(score_cuts, score_cuts[1:])):
            bank = psum.tile([P, last - first], F32, name=f"score_bank{n}", tag=f"bank{n}")
            plane, col = divmod(first, SCORE_N)
            half, word = divmod(first, K_PASS)
            nc.tensor.matmul_mx(
                out=bank[:],
                lhsT=q_codes[:].bitcast(FP8X4),
                lhsT_scale=q_scales[:],
                rhs=key_codes[half][:, word : word + last - first].bitcast(FP8X4),
                rhs_scale=key_scales[4 * plane : P, col : col + last - first],
                start=True,
                stop=True,
            )
            if n % 2 == 0:
                nc.scalar.copy(out=scores[:, first:last], in_=bank[:])
            else:
                nc.vector.tensor_copy(out=scores[:, first:last], in_=bank[:])

        neg_th = sb.tile([P, SLOTS], F32, name="neg_th", tag="after_scores", align_bytes=64)
        nc.vector.tensor_scalar(neg_th[:], th_col[:].to_broadcast([P, SLOTS]), -1.0, None, ALU.mult)

        v_bf = [sb.tile([P, E, PACK], BF16, name=f"v_bf{g}", tag=f"key_codes{1 - g}", align_bytes=64) for g in range(PASSES)]
        v_codes = [sb.tile([P, E], U32, name=f"v_codes{g}", align_bytes=64) for g in range(PASSES)]

        def round_vals(gc):
            g, c = gc
            nc.scalar.copy(
                out=v_bf[g][:, c * OUT_N : (c + 1) * OUT_N, :].rearrange("p (c i) j -> p c j i", i=4),
                in_=v_raw[gc][:].rearrange("p j (c i) -> p c j i", i=4),
            )

        def quantize_vals(g, scales, first, last):
            nc.vector.quantize_mx(
                out=v_codes[g][:, first:last].bitcast(FP8X4),
                scales=scales,
                in_=v_bf[g][:, first:last, :].rearrange("p e j -> p (e j)"),
            )

        listed = sb.tile([P, SLOTS], F32, name="listed")
        nc.vector.tensor_copy(listed[:], scores[:].indirect(offsets[:]))
        round_vals(chunks[0])
        nc.vector.tensor_tensor(placed[:].indirect(offsets[:]), listed[:], neg_th[:], ALU.add)

        passed = v_bf[0][:, OUT_N : OUT_N + SLOTS // PACK, :].rearrange("p e j -> p (e j)")
        row_sum = sb.tile([P, 1], F32, name="row_sum")
        denom = sb.tile([P, 1], F32, name="denom", tag="after_denom", align_bytes=64)
        inv = sb.tile([P, 1], F32, name="inv")
        nc.scalar.activation(passed, listed[:], ACT.Relu, bias=neg_th[:, 0:1], accum_out=row_sum[:])
        nc.scalar.activation(denom[:], row_sum[:], ACT.Identity, bias=reserve_col[:])
        for gc in chunks[1:]:
            round_vals(gc)
        nc.vector.reciprocal(inv[:], denom[:])

        first_bank = psum.tile([P, PACK, Q], F32, name="first_bank", tag="bank5")
        turned = {(0, j): first_bank[:, j, :] for j in range(PACK)}
        for j in range(PACK):
            turned[1, j] = psum.tile([P, Q], F32, name=f"second_bank{j}", tag=f"bank{j}")[:]
        for g in range(PASSES):
            for j in range(PACK):
                nc.tensor.matmul(
                    turned[g, j],
                    lhsT=ground_sb[:, g * K_PASS + j : (g + 1) * K_PASS : PACK],
                    rhs=ident[:],
                    is_transpose=True,
                    start=(g == 1 or j == 0),
                    stop=False,
                )

        dealt = [sb.tile([P, PACK, P], F32, name=f"dealt{g}", tag=f"dealt{g}", align_bytes=64) for g in range(PASSES)]
        for g in range(PASSES):
            step = PACK // 2 if g == 0 else PACK
            for j0 in range(0, PACK, step):
                nc.vector.tensor_scalar(
                    dealt[g][:, j0 : j0 + step, :].rearrange("q j p -> q p j"),
                    placed[:, g * K_PASS : (g + 1) * K_PASS].rearrange("q (p j) -> q p j", j=PACK)[:, :, j0 : j0 + step],
                    0.0,
                    inv[:],
                    ALU.max,
                    ALU.mult,
                )
            for j in range(PACK):
                nc.tensor.matmul(
                    turned[g, j],
                    lhsT=dealt[g][:, j, :],
                    rhs=ident[:],
                    is_transpose=True,
                    start=False,
                    stop=(g == 1 or j == PACK - 1),
                )
        mid_scales = sb.tile([P, 3 * OUT_N], U8, name="mid_scales", tag="after_denom", align_bytes=64)
        quantize_vals(0, mid_scales[:, 0:E], 0, E)
        quantize_vals(1, mid_scales[:, E : E + OUT_N], 0, OUT_N)

        w_bf = [sb.tile([P, Q, PACK], BF16, name=f"w_bf{g}", tag=f"w_bf{g}", align_bytes=64) for g in range(PASSES)]
        w_codes = [sb.tile([P, Q], U32, name=f"w_codes{g}", align_bytes=64) for g in range(PASSES)]
        w_scales = [sb.tile([P, Q], U8, name=f"w_scales{g}", align_bytes=64) for g in range(PASSES)]

        def quantize_weights(g, cols):
            nc.vector.quantize_mx(
                out=w_codes[g][:, cols].bitcast(FP8X4),
                scales=w_scales[g][:, cols],
                in_=w_bf[g][:, cols, :].rearrange("p q j -> p (q j)"),
            )

        nc.vector.tensor_tensor(
            w_bf[0][:],
            first_bank[:].rearrange("p j q -> p q j"),
            fac_cols[:, 0:1, :].to_broadcast([P, Q, PACK]),
            ALU.mult,
        )
        last_scales = sb.tile([P, OUT_N], U8, name="last_scales", tag="dealt0", align_bytes=64)
        quantize_vals(1, last_scales[:], OUT_N, E)
        quantize_weights(0, slice(0, Q))
        w_pairs = sb.tile([P, PACK // 2, Q, 2], BF16, name="w_pairs")
        for j in range(PACK):
            nc.scalar.activation(w_pairs[:, j // 2, :, j % 2], turned[1, j], ACT.Copy, scale=fac_cols[:, 1, j : j + 1])
        pair_words = w_pairs[:].rearrange("p u q e -> p u (q e)").bitcast(F32)
        for half in halves:
            nc.vector.tensor_copy(
                out=w_bf[1][:, half, :].bitcast(F32).rearrange("p (c i) u -> p c u i", i=4),
                in_=pair_words[:, :, half].rearrange("p u (c i) -> p c u i", i=4),
            )
        for half in halves:
            quantize_weights(1, half)
        v_scales = {
            (0, 0): mid_scales[:, 0:OUT_N],
            (0, 1): mid_scales[:, OUT_N:E],
            (1, 0): mid_scales[:, E : E + OUT_N],
            (1, 1): last_scales[:],
        }

        out_cuts = [0, 256, 384, 512]
        spans = list(zip(out_cuts, out_cuts[1:]))
        out_banks = [
            psum.tile([P, last - first], F32, name=f"out_bank{n}", tag=f"bank{(4, 6, 7)[n]}") for n, (first, last) in enumerate(spans)
        ]
        for g in range(PASSES):
            for n, (first, last) in enumerate(spans):
                c, col = divmod(first, OUT_N)
                nc.tensor.matmul_mx(
                    out=out_banks[n][:],
                    lhsT=w_codes[g][:].bitcast(FP8X4),
                    lhsT_scale=w_scales[g][:],
                    rhs=v_codes[g][:, first:last].bitcast(FP8X4),
                    rhs_scale=v_scales[g, c][:, col : col + last - first],
                    start=(g == 0),
                    stop=(g == PASSES - 1),
                )
        result = [sb.tile([P, last - first], F32, name=f"result{n}") for n, (first, last) in enumerate(spans)]
        nc.scalar.copy(out=result[0][:], in_=out_banks[0][:])
        nc.scalar.dma_start(out=out[:, 0:256], in_=result[0][:])
        nc.vector.tensor_copy(out=result[1][:], in_=out_banks[1][:])
        nc.sync.dma_start(out=out[:, 256:384], in_=result[1][:])
        nc.vector.tensor_copy(out=result[2][:], in_=out_banks[2][:])
        nc.sync.dma_start(out=out[:, 384:512], in_=result[2][:])
